import numpy as np
import ml_dtypes


def mxq(x, axis, fmt="e4m3"):
    dtype, down = {"e4m3": (ml_dtypes.float8_e4m3fn, 7), "e5m2": (ml_dtypes.float8_e5m2, 14)}[fmt]
    v = np.moveaxis(np.asarray(x, np.float32).astype(ml_dtypes.bfloat16).astype(np.float64), axis, -1)
    blocks = v.reshape(v.shape[:-1] + (-1, 32))
    amax = np.abs(blocks).max(-1, keepdims=True)
    byte = np.maximum(np.where(amax > 0, np.frexp(amax)[1] - 1 + 127, 0) - down, 1)
    scale = np.exp2(byte - 127.0)
    codes = (blocks / scale).astype(np.float32).astype(dtype).astype(np.float64)
    return np.moveaxis((codes * scale).reshape(v.shape), -1, axis)


WIDE = False


def mx_kscale(k):
    if not WIDE:
        return np.ones(k)
    levels = np.array([10, -10, 5, -5, 0])
    if k % 512:
        return np.exp2(np.random.permutation(np.resize(levels, k // 32))).repeat(32)
    a = np.empty((k // 512, 16))
    for p in range(k // 512):
        a[p, :8] = np.random.permutation(np.resize(levels, 8))
        for g in range(8):
            far = levels[np.abs(levels - a[p, g]) >= 10]
            a[p, g + 8] = far[np.random.randint(len(far))]
    return np.exp2(a.ravel()).repeat(32)


def f64(x):
    return np.asarray(x).astype(np.float64)


def striped(idx):
    return np.tile(np.asarray(idx).reshape(-1, 16).T, (8, 1)).astype(np.uint16)


def unstriped(offs):
    return offs[:16].T.reshape(-1).astype(np.int64)


E2M1 = np.array([0.0, 0.5, 1.0, 1.5, 2.0, 3.0, 4.0, 6.0, -0.0, -0.5, -1.0, -1.5, -2.0, -3.0, -4.0, -6.0])


def pack_weight(w, fmt):
    k, n = w.shape
    w = f64(np.asarray(w, np.float32).astype(ml_dtypes.bfloat16)).reshape(k // 32, 32, n)
    amax = np.abs(w).max(1)
    if fmt == "e4m3":
        byte = np.frexp(amax)[1] - 1 + 127 - 7
    else:
        mant, ex = np.frexp(amax / 6.0)
        byte = np.where(mant > 0.5, ex, ex - 1) + 127
    byte = np.clip(np.where(amax > 0, byte, 1), 1, 254)
    scaled = (w * np.exp2(127.0 - byte)[:, None, :]).reshape(k, n).astype(np.float32)
    by_word = np.ascontiguousarray(scaled.reshape(k // 512, 128, 4, n).transpose(0, 1, 3, 2))
    if fmt == "e4m3":
        words = by_word.astype(ml_dtypes.float8_e4m3fn).view(np.uint8)
    else:
        c = by_word.astype(ml_dtypes.float4_e2m1fn).view(np.uint8) & 0xF
        words = (c[..., 0::2] | (c[..., 1::2] << 4)).reshape(k // 512, 128, 2 * n)
    return np.ascontiguousarray(words), np.ascontiguousarray(byte.astype(np.uint8).reshape(k // 512, 16, n))


def unpack_weight(words, scales, fmt):
    g, _, n = scales.shape
    words = np.ascontiguousarray(words).reshape(g, 128, n, -1)
    if fmt == "e4m3":
        vals = words.view(ml_dtypes.float8_e4m3fn).astype(np.float64)
    else:
        nib = np.empty((g, 128, n, 4), np.uint8)
        nib[..., 0::2] = words & 0xF
        nib[..., 1::2] = words >> 4
        vals = E2M1[nib]
    vals = vals * np.repeat(np.exp2(scales.astype(np.float64) - 127.0), 8, axis=1)[..., None]
    return vals.transpose(0, 1, 3, 2).reshape(g * 512, n)


def softplus(v):
    return np.log(1.0 + np.exp(v))


K, T, J, N = 512, 2048, 512, 512


def setup_inputs():
    n = np.random.standard_normal
    idx = np.random.permutation(T)[:J]
    idx2 = np.random.permutation(T)[:J]
    idx3 = np.random.permutation(T)[:J]
    fk = mx_kscale(K)
    xtp = pack_weight(n((K, T)) / fk[:, None], "e4m3")
    return {
        "xt_words": xtp[0],
        "xt_scales": xtp[1],
        "w": (n((K, N)) * 1 / np.sqrt(K) * fk[:, None]).astype(np.float32),
        "mg": (np.random.uniform(0.2, 1.0, (N, 1))).astype(np.float32),
        "offs": striped(idx),
        "offs2": striped(idx2),
        "offs3": striped(idx3),
    }


def reference(xt_words, xt_scales, w, mg, offs, offs2, offs3):
    idx = unstriped(offs)
    idx2 = unstriped(offs2)
    idx3 = unstriped(offs3)
    xtu = unpack_weight(xt_words, xt_scales, "e4m3")
    wq = mxq(f64(w), 0, "e4m3")
    xtidxg = xtu[:, idx]
    a = wq.T @ xtidxg
    xtidx2g = xtu[:, idx2]
    b = wq.T @ xtidx2g
    xtidx3g = xtu[:, idx3]
    e = wq.T @ xtidx3g
    y = softplus(0.3 * np.square(a - b) - 0.3 * np.square(a - e) + f64(mg))
    return y

@@ -1,0 +1,162 @@
+import math
+from contextlib import ExitStack
+
+import concourse.mybir as mybir
+
+K, T, J, N = 512, 2048, 512, 512
+FLOPS = 3 * 2 * K * N * J
+
+F32 = mybir.dt.float32
+BF16 = mybir.dt.bfloat16
+I32 = mybir.dt.int32
+U32 = mybir.dt.uint32
+U16 = mybir.dt.uint16
+U8 = mybir.dt.uint8
+FP8X4 = mybir.dt.float8_e4m3fn_x4
+ALU = mybir.AluOpType
+ACT = mybir.ActivationFunctionType
+
+P = 128
+PACK = 4
+HALF = J // 2
+TILES = N // P
+GAP_WEIGHT = 0.3
+EXP_CAP = 2.0**50
+
+
+def tile_list_anchor_near_and_far_kernel(tc, xt_words, xt_scales, w, mg, offs, offs2, offs3, out):
+    nc = tc.nc
+    with ExitStack() as ctx:
+        held = ctx.enter_context(tc.tile_pool(name="held", bufs=1))
+        work = ctx.enter_context(tc.tile_pool(name="work", bufs=3))
+        gaps = ctx.enter_context(tc.psum_pool(name="gaps", bufs=7))
+        near = ctx.enter_context(tc.psum_pool(name="near", bufs=1))
+
+        table_scales = held.tile([P, T], U8, name="table_scales", align_bytes=64)
+        nc.vector.memset(table_scales[:].bitcast(I32), 0)
+        lists = []
+        for i, src in enumerate((offs, offs2, offs3)):
+            lst = held.tile([P, J // 16], U16, name="list%d" % i)
+            nc.sync.dma_start(lst[:], src)
+            lists.append(lst)
+        for q in range(4):
+            nc.sync.dma_start(
+                table_scales[32 * q : 32 * q + 4, :].bitcast(I32), xt_scales[0, 4 * q : 4 * q + 4, :].bitcast(I32)
+            )
+        w_rows = w.rearrange("(p j) n -> p j n", j=PACK)
+        w_raw = []
+        for h in range(2):
+            raw = held.tile([P, PACK, N // 2], F32, name="w_raw%d" % h)
+            nc.sync.dma_start(raw[:], w_rows[:, :, h * (N // 2) : (h + 1) * (N // 2)])
+            w_raw.append(raw)
+        table_words = held.tile([P, T], I32, name="table_words", align_bytes=64)
+        nc.sync.dma_start(table_words[:], xt_words[0].rearrange("p n t -> p (n t)").bitcast(I32))
+        margin = held.tile([P, TILES], F32, name="margin")
+        with nc.allow_non_contiguous_dma(reason="one margin a partition"):
+            nc.sync.dma_start(margin[:], mg.rearrange("(t p) o -> p (t o)", p=P))
+
+        picked_scales = []
+        for i in range(3):
+            s = held.tile([P, J], U8, name="picked_scales%d" % i, align_bytes=64)
+            nc.vector.tensor_copy(s[:], table_scales[:].indirect(lists[i][:]))
+            picked_scales.append(s)
+
+        def quantise(name, raw, sign):
+            cols = raw.shape[2]
+            grouped = held.tile([P, cols, PACK], BF16, name=name + "_bf16", tag=name + "_bf16", align_bytes=64)
+            if sign > 0:
+                nc.scalar.activation(
+                    grouped[:].rearrange("p (c i) j -> p c j i", i=4),
+                    raw.rearrange("p j (c i) -> p c j i", i=4),
+                    ACT.Copy,
+                )
+            else:
+                nc.gpsimd.tensor_scalar(grouped[:], raw.rearrange("p j c -> p c j"), -1.0, 0.0, ALU.mult, ALU.add)
+            codes = held.tile([P, cols], U32, name=name + "_codes", align_bytes=64)
+            scales = held.tile([P, cols], U8, name=name + "_scales", align_bytes=64)
+            nc.vector.quantize_mx(
+                out=codes[:].bitcast(FP8X4), scales=scales[:], in_=grouped[:].rearrange("p c j -> p (c j)")
+            )
+            return [(codes[:, c : c + P], scales[:, c : c + P]) for c in range(0, cols, P)]
+
+        plus = quantise("w_plus0", w_raw[0][:], 1.0)
+        minus = [None] + quantise("w_minus0", w_raw[0][:, :, P:], -1.0)
+        plus = plus + quantise("w_plus1", w_raw[1][:], 1.0)
+        minus = minus + quantise("w_minus1", w_raw[1][:], -1.0)
+
+        picked = {}
+        first_words = held.tile([P, HALF], U32, name="first_words", tag="w_plus1_bf16", align_bytes=64)
+        later_words = held.tile([P, 5, HALF], U32, name="later_words", tag="w_minus1_bf16", align_bytes=64)
+        for h in range(2):
+            for i in range(3):
+                x = first_words[:] if h + i == 0 else later_words[:, 3 * h + i - 1, :]
+                cols = slice(h * HALF // 16, (h + 1) * HALF // 16)
+                nc.vector.tensor_copy(x, table_words[:].bitcast(U32).indirect(lists[i][:, cols]))
+                picked[i, h] = (x, picked_scales[i][:, h * HALF : (h + 1) * HALF])
+
+        def product(dst, weight, tokens, start, stop):
+            nc.tensor.matmul_mx(
+                out=dst,
+                lhsT=weight[0].bitcast(FP8X4),
+                lhsT_scale=weight[1],
+                rhs=tokens[0].bitcast(FP8X4),
+                rhs_scale=tokens[1],
+                start=start,
+                stop=stop,
+            )
+
+        z = held.tile([P, TILES, J], F32, name="z")
+        ex = held.tile([P, TILES, J], F32, name="ex")
+        near_bank = near.tile([P, 2, HALF], F32, name="near_bank")
+        last = TILES - 1
+
+        def exp_of(t, cols):
+            nc.scalar.activation(ex[:, t, cols], z[:, t, cols], ACT.Exp, bias=margin[:, t : t + 1])
+
+        def squares_unit(t, h):
+            cols = slice(h * HALF, (h + 1) * HALF)
+            bank = gaps.tile([P, 2, HALF], F32, name="bank")
+            for g in range(2):
+                product(bank[:, g, :], plus[t], picked[0, h], True, False)
+                product(bank[:, g, :], minus[t], picked[1 + g, h], False, True)
+            sq = work.tile([P, 2, HALF], F32, name="sq")
+            nc.scalar.activation(sq[:], bank[:], ACT.Square, scale=math.sqrt(GAP_WEIGHT))
+            nc.gpsimd.tensor_tensor(z[:, t, cols], sq[:, 0, :], sq[:, 1, :], ALU.subtract)
+            exp_of(t, cols)
+
+        def product_unit(t, h):
+            cols = slice(h * HALF, (h + 1) * HALF)
+            bank = gaps.tile([P, 2, HALF], F32, name="bank")
+            product(near_bank[:, h, :], plus[t], picked[1, h], True, True)
+            product(bank[:, 0, :], plus[t], picked[0, h], True, True)
+            product(bank[:, 1, :], plus[t], picked[2, h], True, True)
+            b = work.tile([P, HALF], F32, name="b")
+            nc.vector.tensor_copy(b[:], near_bank[:, h, :])
+            u = work.tile([P, HALF], F32, name="u")
+            nc.vector.tensor_tensor(u[:], bank[:, 1, :], b[:], ALU.subtract)
+            s = work.tile([P, HALF], F32, name="s")
+            nc.vector.scalar_tensor_tensor(s[:], bank[:, 0, :], 2.0, b[:], ALU.mult, ALU.subtract)
+            v = work.tile([P, HALF], F32, name="v")
+            nc.vector.tensor_tensor(v[:], s[:], bank[:, 1, :], ALU.subtract)
+            nc.vector.scalar_tensor_tensor(z[:, t, cols], u[:], GAP_WEIGHT, v[:], ALU.mult, ALU.mult)
+
+        for t in range(1, TILES):
+            squares_unit(t, 0)
+        product_unit(0, 0)
+        squares_unit(1, 1)
+        product_unit(0, 1)
+        for t in range(2, TILES):
+            squares_unit(t, 1)
+        exp_of(0, slice(0, J))
+
+        one_plus = held.tile([P, TILES, J], F32, name="one_plus")
+        nc.vector.tensor_scalar(
+            one_plus[:].rearrange("p t j -> p (t j)"), ex[:].rearrange("p t j -> p (t j)"), EXP_CAP, 1.0, ALU.min, ALU.add
+        )
+        pieces = [(t, 0, J) for t in range(last)] + [(last, 0, HALF), (last, HALF, J)]
+        for t, c0, c1 in pieces:
+            soft = held.tile([P, c1 - c0], F32, name="soft%d_%d" % (t, c0))
+            nc.scalar.activation(soft[:], one_plus[:, t, c0:c1], ACT.Ln)
+            y = held.tile([P, c1 - c0], F32, name="y%d_%d" % (t, c0))
+            nc.vector.scalar_tensor_tensor(y[:], z[:, t, c0:c1], margin[:, t : t + 1], soft[:], ALU.add, ALU.max)
+            nc.sync.dma_start(out[t * P : (t + 1) * P, c0:c1], y[:])

@@ -64,14 +64,12 @@ def tile_list_anchor_near_and_far_kernel(tc, xt_words, xt_scales, w, mg, offs, o
         def quantise(name, raw, sign):
             cols = raw.shape[2]
             grouped = held.tile([P, cols, PACK], BF16, name=name + "_bf16", tag=name + "_bf16", align_bytes=64)
-            if sign > 0:
-                nc.scalar.activation(
-                    grouped[:].rearrange("p (c i) j -> p c j i", i=4),
-                    raw.rearrange("p j (c i) -> p c j i", i=4),
-                    ACT.Copy,
-                )
-            else:
-                nc.gpsimd.tensor_scalar(grouped[:], raw.rearrange("p j c -> p c j"), -1.0, 0.0, ALU.mult, ALU.add)
+            nc.scalar.activation(
+                grouped[:].rearrange("p (c i) j -> p c j i", i=4),
+                raw.rearrange("p j (c i) -> p c j i", i=4),
+                ACT.Copy,
+                scale=sign,
+            )
             codes = held.tile([P, cols], U32, name=name + "_codes", align_bytes=64)
             scales = held.tile([P, cols], U8, name=name + "_scales", align_bytes=64)
             nc.vector.quantize_mx(
@@ -80,16 +78,16 @@ def tile_list_anchor_near_and_far_kernel(tc, xt_words, xt_scales, w, mg, offs, o
             return [(codes[:, c : c + P], scales[:, c : c + P]) for c in range(0, cols, P)]
 
         plus = quantise("w_plus0", w_raw[0][:], 1.0)
-        minus = [None] + quantise("w_minus0", w_raw[0][:, :, P:], -1.0)
+        minus = quantise("w_minus0", w_raw[0][:], -1.0)
         plus = plus + quantise("w_plus1", w_raw[1][:], 1.0)
-        minus = minus + quantise("w_minus1", w_raw[1][:], -1.0)
+        minus = minus + quantise("w_minus1", w_raw[1][:, :, 0:P], -1.0)
 
         picked = {}
-        first_words = held.tile([P, HALF], U32, name="first_words", tag="w_plus1_bf16", align_bytes=64)
-        later_words = held.tile([P, 5, HALF], U32, name="later_words", tag="w_minus1_bf16", align_bytes=64)
+        first_words = held.tile([P, 3, HALF], U32, name="first_words", align_bytes=64)
+        later_words = held.tile([P, 3, HALF], U32, name="later_words", tag="w_minus1_bf16", align_bytes=64)
         for h in range(2):
             for i in range(3):
-                x = first_words[:] if h + i == 0 else later_words[:, 3 * h + i - 1, :]
+                x = (first_words, later_words)[h][:, i, :]
                 cols = slice(h * HALF // 16, (h + 1) * HALF // 16)
                 nc.vector.tensor_copy(x, table_words[:].bitcast(U32).indirect(lists[i][:, cols]))
                 picked[i, h] = (x, picked_scales[i][:, h * HALF : (h + 1) * HALF])
@@ -113,15 +111,23 @@ def tile_list_anchor_near_and_far_kernel(tc, xt_words, xt_scales, w, mg, offs, o
         def exp_of(t, cols):
             nc.scalar.activation(ex[:, t, cols], z[:, t, cols], ACT.Exp, bias=margin[:, t : t + 1])
 
-        def squares_unit(t, h):
-            cols = slice(h * HALF, (h + 1) * HALF)
+        sq = held.tile([P, last, 2, 2, HALF], F32, name="sq")
+
+        def squares(t, h):
             bank = gaps.tile([P, 2, HALF], F32, name="bank")
             for g in range(2):
                 product(bank[:, g, :], plus[t], picked[0, h], True, False)
                 product(bank[:, g, :], minus[t], picked[1 + g, h], False, True)
-            sq = work.tile([P, 2, HALF], F32, name="sq")
-            nc.scalar.activation(sq[:], bank[:], ACT.Square, scale=math.sqrt(GAP_WEIGHT))
-            nc.gpsimd.tensor_tensor(z[:, t, cols], sq[:, 0, :], sq[:, 1, :], ALU.subtract)
+            nc.scalar.activation(sq[:, t, h, :, :], bank[:], ACT.Square, scale=math.sqrt(GAP_WEIGHT))
+
+        def difference(t, h0, h1):
+            cols = slice(h0 * HALF, h1 * HALF)
+            nc.vector.tensor_tensor(
+                z[:, t, cols].rearrange("p (h c) -> p h c", c=HALF),
+                sq[:, t, h0:h1, 0, :],
+                sq[:, t, h0:h1, 1, :],
+                ALU.subtract,
+            )
             exp_of(t, cols)
 
         def product_unit(t, h):
@@ -131,23 +137,25 @@ def tile_list_anchor_near_and_far_kernel(tc, xt_words, xt_scales, w, mg, offs, o
             product(bank[:, 0, :], plus[t], picked[0, h], True, True)
             product(bank[:, 1, :], plus[t], picked[2, h], True, True)
             b = work.tile([P, HALF], F32, name="b")
-            nc.vector.tensor_copy(b[:], near_bank[:, h, :])
-            u = work.tile([P, HALF], F32, name="u")
-            nc.vector.tensor_tensor(u[:], bank[:, 1, :], b[:], ALU.subtract)
-            s = work.tile([P, HALF], F32, name="s")
-            nc.vector.scalar_tensor_tensor(s[:], bank[:, 0, :], 2.0, b[:], ALU.mult, ALU.subtract)
+            nc.scalar.copy(b[:], near_bank[:, h, :])
+            du = work.tile([P, 2, HALF], F32, name="du")
+            nc.vector.tensor_tensor(du[:], bank[:], b[:].unsqueeze(1).to_broadcast([P, 2, HALF]), ALU.subtract)
             v = work.tile([P, HALF], F32, name="v")
-            nc.vector.tensor_tensor(v[:], s[:], bank[:, 1, :], ALU.subtract)
-            nc.vector.scalar_tensor_tensor(z[:, t, cols], u[:], GAP_WEIGHT, v[:], ALU.mult, ALU.mult)
+            nc.vector.scalar_tensor_tensor(v[:], du[:, 0, :], 2.0, du[:, 1, :], ALU.mult, ALU.subtract)
+            nc.vector.scalar_tensor_tensor(z[:, t, cols], du[:, 1, :], GAP_WEIGHT, v[:], ALU.mult, ALU.mult)
 
-        for t in range(1, TILES):
-            squares_unit(t, 0)
-        product_unit(0, 0)
-        squares_unit(1, 1)
-        product_unit(0, 1)
-        for t in range(2, TILES):
-            squares_unit(t, 1)
-        exp_of(0, slice(0, J))
+        for t in range(last):
+            squares(t, 0)
+        product_unit(last, 0)
+        difference(last - 1, 0, 1)
+        squares(0, 1)
+        product_unit(last, 1)
+        difference(0, 0, 2)
+        squares(1, 1)
+        squares(2, 1)
+        exp_of(last, slice(0, J))
+        difference(1, 0, 2)
+        difference(2, 1, 2)
 
         one_plus = held.tile([P, TILES, J], F32, name="one_plus")
         nc.vector.tensor_scalar(

@@ -113,49 +113,49 @@ def tile_list_anchor_near_and_far_kernel(tc, xt_words, xt_scales, w, mg, offs, o
 
         sq = held.tile([P, last, 2, 2, HALF], F32, name="sq")
 
-        def squares(t, h):
-            bank = gaps.tile([P, 2, HALF], F32, name="bank")
-            for g in range(2):
-                product(bank[:, g, :], plus[t], picked[0, h], True, False)
-                product(bank[:, g, :], minus[t], picked[1 + g, h], False, True)
+        def gap_passes(h, banks, tiles):
+            for t in tiles:
+                product(banks[t][:, 0, :], plus[t], picked[0, h], True, t == last)
+                if t < last:
+                    product(banks[t][:, 1, :], plus[t], picked[0, h], False, False)
+            for t in tiles:
+                if t < last:
+                    product(banks[t][:, 0, :], minus[t], picked[1, h], False, False)
+                else:
+                    product(near_bank[:, h, :], plus[t], picked[1, h], True, True)
+            for t in tiles:
+                product(banks[t][:, 1, :], (minus[t] if t < last else plus[t]), picked[2, h], t == last, True)
+
+        def squares(t, h, bank):
             nc.scalar.activation(sq[:, t, h, :, :], bank[:], ACT.Square, scale=math.sqrt(GAP_WEIGHT))
 
-        def difference(t, h0, h1):
-            cols = slice(h0 * HALF, h1 * HALF)
-            nc.vector.tensor_tensor(
-                z[:, t, cols].rearrange("p (h c) -> p h c", c=HALF),
-                sq[:, t, h0:h1, 0, :],
-                sq[:, t, h0:h1, 1, :],
-                ALU.subtract,
-            )
+        def difference(t, h):
+            cols = slice(h * HALF, (h + 1) * HALF)
+            nc.gpsimd.tensor_tensor(z[:, t, cols], sq[:, t, h, 0, :], sq[:, t, h, 1, :], ALU.subtract)
             exp_of(t, cols)
 
-        def product_unit(t, h):
+        def product_unit(t, h, bank):
             cols = slice(h * HALF, (h + 1) * HALF)
-            bank = gaps.tile([P, 2, HALF], F32, name="bank")
-            product(near_bank[:, h, :], plus[t], picked[1, h], True, True)
-            product(bank[:, 0, :], plus[t], picked[0, h], True, True)
-            product(bank[:, 1, :], plus[t], picked[2, h], True, True)
             b = work.tile([P, HALF], F32, name="b")
-            nc.scalar.copy(b[:], near_bank[:, h, :])
-            du = work.tile([P, 2, HALF], F32, name="du")
-            nc.vector.tensor_tensor(du[:], bank[:], b[:].unsqueeze(1).to_broadcast([P, 2, HALF]), ALU.subtract)
+            nc.vector.tensor_copy(b[:], near_bank[:, h, :])
+            u = work.tile([P, HALF], F32, name="u")
+            nc.vector.tensor_tensor(u[:], bank[:, 1, :], b[:], ALU.subtract)
+            s = work.tile([P, HALF], F32, name="s")
+            nc.vector.scalar_tensor_tensor(s[:], bank[:, 0, :], 2.0, b[:], ALU.mult, ALU.subtract)
             v = work.tile([P, HALF], F32, name="v")
-            nc.vector.scalar_tensor_tensor(v[:], du[:, 0, :], 2.0, du[:, 1, :], ALU.mult, ALU.subtract)
-            nc.vector.scalar_tensor_tensor(z[:, t, cols], du[:, 1, :], GAP_WEIGHT, v[:], ALU.mult, ALU.mult)
+            nc.vector.tensor_tensor(v[:], s[:], bank[:, 1, :], ALU.subtract)
+            nc.vector.scalar_tensor_tensor(z[:, t, cols], u[:], GAP_WEIGHT, v[:], ALU.mult, ALU.mult)
 
-        for t in range(last):
-            squares(t, 0)
-        product_unit(last, 0)
-        difference(last - 1, 0, 1)
-        squares(0, 1)
-        product_unit(last, 1)
-        difference(0, 0, 2)
-        squares(1, 1)
-        squares(2, 1)
+        for h, groups in enumerate((([0, 1], [2], [last]), ([0, 1, 2, last],))):
+            banks = [gaps.tile([P, 2, HALF], F32, name="bank") for t in range(TILES)]
+            for tiles in groups:
+                gap_passes(h, banks, tiles)
+            for t in range(last):
+                squares(t, h, banks[t])
+            for t in range(last):
+                difference(t, h)
+            product_unit(last, h, banks[last])
         exp_of(last, slice(0, J))
-        difference(1, 0, 2)
-        difference(2, 1, 2)
 
         one_plus = held.tile([P, TILES, J], F32, name="one_plus")
         nc.vector.tensor_scalar(

@@ -40,17 +40,15 @@ def tile_list_anchor_near_and_far_kernel(tc, xt_words, xt_scales, w, mg, offs, o
             nc.sync.dma_start(lst[:], src)
             lists.append(lst)
         for q in range(4):
-            nc.sync.dma_start(
+            (nc.sync, nc.scalar)[q % 2].dma_start(
                 table_scales[32 * q : 32 * q + 4, :].bitcast(I32), xt_scales[0, 4 * q : 4 * q + 4, :].bitcast(I32)
             )
         w_rows = w.rearrange("(p j) n -> p j n", j=PACK)
-        w_raw = []
-        for h in range(2):
-            raw = held.tile([P, PACK, N // 2], F32, name="w_raw%d" % h)
-            nc.sync.dma_start(raw[:], w_rows[:, :, h * (N // 2) : (h + 1) * (N // 2)])
-            w_raw.append(raw)
+        w_raw = [held.tile([P, PACK, N // 2], F32, name="w_raw%d" % h) for h in range(2)]
         table_words = held.tile([P, T], I32, name="table_words", align_bytes=64)
+        nc.sync.dma_start(w_raw[0][:], w_rows[:, :, 0 : N // 2])
         nc.sync.dma_start(table_words[:], xt_words[0].rearrange("p n t -> p (n t)").bitcast(I32))
+        nc.sync.dma_start(w_raw[1][:], w_rows[:, :, N // 2 : N])
         margin = held.tile([P, TILES], F32, name="margin")
         with nc.allow_non_contiguous_dma(reason="one margin a partition"):
             nc.sync.dma_start(margin[:], mg.rearrange("(t p) o -> p (t o)", p=P))
@@ -79,18 +77,23 @@ def tile_list_anchor_near_and_far_kernel(tc, xt_words, xt_scales, w, mg, offs, o
 
         plus = quantise("w_plus0", w_raw[0][:], 1.0)
         minus = quantise("w_minus0", w_raw[0][:], -1.0)
+        picked = {}
+
+        def gather_words(i, h, words):
+            cols = slice(h * HALF // 16, (h + 1) * HALF // 16)
+            nc.vector.tensor_copy(words, table_words[:].bitcast(U32).indirect(lists[i][:, cols]))
+            picked[i, h] = (words, picked_scales[i][:, h * HALF : (h + 1) * HALF])
+
+        anchor_words = held.tile([P, HALF], U32, name="anchor_words", align_bytes=64)
+        gather_words(0, 0, anchor_words[:])
+        middle_words = held.tile([P, 3, HALF], U32, name="middle_words", tag="w_minus0_bf16", align_bytes=64)
+        for slot, (i, h) in enumerate(((1, 0), (2, 0), (0, 1))):
+            gather_words(i, h, middle_words[:, slot, :])
         plus = plus + quantise("w_plus1", w_raw[1][:], 1.0)
         minus = minus + quantise("w_minus1", w_raw[1][:, :, 0:P], -1.0)
-
-        picked = {}
-        first_words = held.tile([P, 3, HALF], U32, name="first_words", align_bytes=64)
-        later_words = held.tile([P, 3, HALF], U32, name="later_words", tag="w_minus1_bf16", align_bytes=64)
-        for h in range(2):
-            for i in range(3):
-                x = (first_words, later_words)[h][:, i, :]
-                cols = slice(h * HALF // 16, (h + 1) * HALF // 16)
-                nc.vector.tensor_copy(x, table_words[:].bitcast(U32).indirect(lists[i][:, cols]))
-                picked[i, h] = (x, picked_scales[i][:, h * HALF : (h + 1) * HALF])
+        last_words = held.tile([P, 2, HALF], U32, name="last_words", tag="w_minus1_bf16", align_bytes=64)
+        for i in range(1, 3):
+            gather_words(i, 1, last_words[:, i - 1, :])
 
         def product(dst, weight, tokens, start, stop):
             nc.tensor.matmul_mx(
@@ -121,40 +124,48 @@ def tile_list_anchor_near_and_far_kernel(tc, xt_words, xt_scales, w, mg, offs, o
             for t in tiles:
                 if t < last:
                     product(banks[t][:, 0, :], minus[t], picked[1, h], False, False)
-                else:
-                    product(near_bank[:, h, :], plus[t], picked[1, h], True, True)
             for t in tiles:
                 product(banks[t][:, 1, :], (minus[t] if t < last else plus[t]), picked[2, h], t == last, True)
+            if last in tiles:
+                product(near_bank[:, h, :], plus[last], picked[1, h], True, True)
 
         def squares(t, h, bank):
             nc.scalar.activation(sq[:, t, h, :, :], bank[:], ACT.Square, scale=math.sqrt(GAP_WEIGHT))
 
-        def difference(t, h):
+        def difference(engine, t, h):
             cols = slice(h * HALF, (h + 1) * HALF)
-            nc.gpsimd.tensor_tensor(z[:, t, cols], sq[:, t, h, 0, :], sq[:, t, h, 1, :], ALU.subtract)
-            exp_of(t, cols)
+            engine.tensor_tensor(z[:, t, cols], sq[:, t, h, 0, :], sq[:, t, h, 1, :], ALU.subtract)
 
         def product_unit(t, h, bank):
             cols = slice(h * HALF, (h + 1) * HALF)
             b = work.tile([P, HALF], F32, name="b")
             nc.vector.tensor_copy(b[:], near_bank[:, h, :])
-            u = work.tile([P, HALF], F32, name="u")
-            nc.vector.tensor_tensor(u[:], bank[:, 1, :], b[:], ALU.subtract)
-            s = work.tile([P, HALF], F32, name="s")
-            nc.vector.scalar_tensor_tensor(s[:], bank[:, 0, :], 2.0, b[:], ALU.mult, ALU.subtract)
+            du = work.tile([P, 2, HALF], F32, name="du")
+            nc.vector.tensor_tensor(du[:], bank[:], b[:].unsqueeze(1).to_broadcast([P, 2, HALF]), ALU.subtract)
             v = work.tile([P, HALF], F32, name="v")
-            nc.vector.tensor_tensor(v[:], s[:], bank[:, 1, :], ALU.subtract)
-            nc.vector.scalar_tensor_tensor(z[:, t, cols], u[:], GAP_WEIGHT, v[:], ALU.mult, ALU.mult)
+            nc.vector.scalar_tensor_tensor(v[:], du[:, 0, :], 2.0, du[:, 1, :], ALU.mult, ALU.subtract)
+            nc.vector.scalar_tensor_tensor(z[:, t, cols], du[:, 1, :], GAP_WEIGHT, v[:], ALU.mult, ALU.mult)
 
-        for h, groups in enumerate((([0, 1], [2], [last]), ([0, 1, 2, last],))):
-            banks = [gaps.tile([P, 2, HALF], F32, name="bank") for t in range(TILES)]
-            for tiles in groups:
-                gap_passes(h, banks, tiles)
-            for t in range(last):
-                squares(t, h, banks[t])
-            for t in range(last):
-                difference(t, h)
-            product_unit(last, h, banks[last])
+        banks = [gaps.tile([P, 2, HALF], F32, name="bank") for t in range(TILES)]
+        for tiles in ([0, 1], [2], [last]):
+            gap_passes(0, banks, tiles)
+        for t in range(last):
+            squares(t, 0, banks[t])
+        for t in range(last):
+            difference(nc.gpsimd, t, 0)
+        exp_of(0, slice(0, HALF))
+        product_unit(last, 0, banks[last])
+        banks = [gaps.tile([P, 2, HALF], F32, name="bank") for t in range(TILES)]
+        for tiles in ([0, 1], [2], [last]):
+            gap_passes(1, banks, tiles)
+        for t in range(last):
+            squares(t, 1, banks[t])
+        difference(nc.gpsimd, 0, 1)
+        exp_of(0, slice(HALF, J))
+        for t in range(1, last):
+            difference(nc.vector, t, 1)
+            exp_of(t, slice(0, J))
+        product_unit(last, 1, banks[last])
         exp_of(last, slice(0, J))
 
         one_plus = held.tile([P, TILES, J], F32, name="one_plus")

@@ -40,7 +40,7 @@ def tile_list_anchor_near_and_far_kernel(tc, xt_words, xt_scales, w, mg, offs, o
             nc.sync.dma_start(lst[:], src)
             lists.append(lst)
         for q in range(4):
-            (nc.sync, nc.scalar)[q % 2].dma_start(
+            nc.sync.dma_start(
                 table_scales[32 * q : 32 * q + 4, :].bitcast(I32), xt_scales[0, 4 * q : 4 * q + 4, :].bitcast(I32)
             )
         w_rows = w.rearrange("(p j) n -> p j n", j=PACK)

import math
from contextlib import ExitStack

import concourse.mybir as mybir

K, T, J, N = 512, 2048, 512, 512
FLOPS = 3 * 2 * K * N * J

F32 = mybir.dt.float32
BF16 = mybir.dt.bfloat16
I32 = mybir.dt.int32
U32 = mybir.dt.uint32
U16 = mybir.dt.uint16
U8 = mybir.dt.uint8
FP8X4 = mybir.dt.float8_e4m3fn_x4
ALU = mybir.AluOpType
ACT = mybir.ActivationFunctionType

P = 128
PACK = 4
HALF = J // 2
TILES = N // P
GAP_WEIGHT = 0.3
EXP_CAP = 2.0**50


def tile_list_anchor_near_and_far_kernel(tc, xt_words, xt_scales, w, mg, offs, offs2, offs3, out):
    nc = tc.nc
    with ExitStack() as ctx:
        held = ctx.enter_context(tc.tile_pool(name="held", bufs=1))
        work = ctx.enter_context(tc.tile_pool(name="work", bufs=3))
        gaps = ctx.enter_context(tc.psum_pool(name="gaps", bufs=7))
        near = ctx.enter_context(tc.psum_pool(name="near", bufs=1))

        table_scales = held.tile([P, T], U8, name="table_scales", align_bytes=64)
        nc.vector.memset(table_scales[:].bitcast(I32), 0)
        lists = []
        for i, src in enumerate((offs, offs2, offs3)):
            lst = held.tile([P, J // 16], U16, name="list%d" % i)
            nc.sync.dma_start(lst[:], src)
            lists.append(lst)
        for q in range(4):
            nc.sync.dma_start(
                table_scales[32 * q : 32 * q + 4, :].bitcast(I32), xt_scales[0, 4 * q : 4 * q + 4, :].bitcast(I32)
            )
        w_rows = w.rearrange("(p j) n -> p j n", j=PACK)
        w_raw = [held.tile([P, PACK, N // 2], F32, name="w_raw%d" % h) for h in range(2)]
        table_words = held.tile([P, T], I32, name="table_words", align_bytes=64)
        nc.sync.dma_start(w_raw[0][:], w_rows[:, :, 0 : N // 2])
        nc.sync.dma_start(table_words[:], xt_words[0].rearrange("p n t -> p (n t)").bitcast(I32))
        nc.sync.dma_start(w_raw[1][:], w_rows[:, :, N // 2 : N])
        margin = held.tile([P, TILES], F32, name="margin")
        with nc.allow_non_contiguous_dma(reason="one margin a partition"):
            nc.sync.dma_start(margin[:], mg.rearrange("(t p) o -> p (t o)", p=P))

        picked_scales = []
        for i in range(3):
            s = held.tile([P, J], U8, name="picked_scales%d" % i, align_bytes=64)
            nc.vector.tensor_copy(s[:], table_scales[:].indirect(lists[i][:]))
            picked_scales.append(s)

        def quantise(name, raw, sign):
            cols = raw.shape[2]
            grouped = held.tile([P, cols, PACK], BF16, name=name + "_bf16", tag=name + "_bf16", align_bytes=64)
            nc.scalar.activation(
                grouped[:].rearrange("p (c i) j -> p c j i", i=4),
                raw.rearrange("p j (c i) -> p c j i", i=4),
                ACT.Copy,
                scale=sign,
            )
            codes = held.tile([P, cols], U32, name=name + "_codes", align_bytes=64)
            scales = held.tile([P, cols], U8, name=name + "_scales", align_bytes=64)
            nc.vector.quantize_mx(
                out=codes[:].bitcast(FP8X4), scales=scales[:], in_=grouped[:].rearrange("p c j -> p (c j)")
            )
            return [(codes[:, c : c + P], scales[:, c : c + P]) for c in range(0, cols, P)]

        plus = quantise("w_plus0", w_raw[0][:], 1.0)
        minus = quantise("w_minus0", w_raw[0][:], -1.0)
        picked = {}

        def gather_words(i, h, words):
            cols = slice(h * HALF // 16, (h + 1) * HALF // 16)
            nc.vector.tensor_copy(words, table_words[:].bitcast(U32).indirect(lists[i][:, cols]))
            picked[i, h] = (words, picked_scales[i][:, h * HALF : (h + 1) * HALF])

        anchor_words = held.tile([P, HALF], U32, name="anchor_words", align_bytes=64)
        gather_words(0, 0, anchor_words[:])
        middle_words = held.tile([P, 3, HALF], U32, name="middle_words", tag="w_minus0_bf16", align_bytes=64)
        for slot, (i, h) in enumerate(((1, 0), (2, 0), (0, 1))):
            gather_words(i, h, middle_words[:, slot, :])
        plus = plus + quantise("w_plus1", w_raw[1][:], 1.0)
        minus = minus + quantise("w_minus1", w_raw[1][:, :, 0:P], -1.0)
        last_words = held.tile([P, 2, HALF], U32, name="last_words", tag="w_minus1_bf16", align_bytes=64)
        for i in range(1, 3):
            gather_words(i, 1, last_words[:, i - 1, :])

        def product(dst, weight, tokens, start, stop):
            nc.tensor.matmul_mx(
                out=dst,
                lhsT=weight[0].bitcast(FP8X4),
                lhsT_scale=weight[1],
                rhs=tokens[0].bitcast(FP8X4),
                rhs_scale=tokens[1],
                start=start,
                stop=stop,
            )

        z = held.tile([P, TILES, J], F32, name="z")
        ex = held.tile([P, TILES, J], F32, name="ex")
        near_bank = near.tile([P, 2, HALF], F32, name="near_bank")
        last = TILES - 1

        def exp_of(t, cols):
            nc.scalar.activation(ex[:, t, cols], z[:, t, cols], ACT.Exp, bias=margin[:, t : t + 1])

        sq = held.tile([P, last, 2, 2, HALF], F32, name="sq")

        def gap_passes(h, banks, tiles):
            for t in tiles:
                product(banks[t][:, 0, :], plus[t], picked[0, h], True, t == last)
                if t < last:
                    product(banks[t][:, 1, :], plus[t], picked[0, h], False, False)
            for t in tiles:
                if t < last:
                    product(banks[t][:, 0, :], minus[t], picked[1, h], False, False)
            for t in tiles:
                product(banks[t][:, 1, :], (minus[t] if t < last else plus[t]), picked[2, h], t == last, True)
            if last in tiles:
                product(near_bank[:, h, :], plus[last], picked[1, h], True, True)

        def squares(t, h, bank):
            nc.scalar.activation(sq[:, t, h, :, :], bank[:], ACT.Square, scale=math.sqrt(GAP_WEIGHT))

        def difference(engine, t, h):
            cols = slice(h * HALF, (h + 1) * HALF)
            engine.tensor_tensor(z[:, t, cols], sq[:, t, h, 0, :], sq[:, t, h, 1, :], ALU.subtract)

        def product_unit(t, h, bank):
            cols = slice(h * HALF, (h + 1) * HALF)
            b = work.tile([P, HALF], F32, name="b")
            nc.vector.tensor_copy(b[:], near_bank[:, h, :])
            du = work.tile([P, 2, HALF], F32, name="du")
            nc.vector.tensor_tensor(du[:], bank[:], b[:].unsqueeze(1).to_broadcast([P, 2, HALF]), ALU.subtract)
            v = work.tile([P, HALF], F32, name="v")
            nc.vector.scalar_tensor_tensor(v[:], du[:, 0, :], 2.0, du[:, 1, :], ALU.mult, ALU.subtract)
            nc.vector.scalar_tensor_tensor(z[:, t, cols], du[:, 1, :], GAP_WEIGHT, v[:], ALU.mult, ALU.mult)

        banks = [gaps.tile([P, 2, HALF], F32, name="bank") for t in range(TILES)]
        for tiles in ([0, 1], [2], [last]):
            gap_passes(0, banks, tiles)
        for t in range(last):
            squares(t, 0, banks[t])
        for t in range(last):
            difference(nc.gpsimd, t, 0)
        exp_of(0, slice(0, HALF))
        product_unit(last, 0, banks[last])
        banks = [gaps.tile([P, 2, HALF], F32, name="bank") for t in range(TILES)]
        for tiles in ([0, 1], [2], [last]):
            gap_passes(1, banks, tiles)
        for t in range(last):
            squares(t, 1, banks[t])
        difference(nc.gpsimd, 0, 1)
        exp_of(0, slice(HALF, J))
        for t in range(1, last):
            difference(nc.vector, t, 1)
            exp_of(t, slice(0, J))
        product_unit(last, 1, banks[last])
        exp_of(last, slice(0, J))

        one_plus = held.tile([P, TILES, J], F32, name="one_plus")
        nc.vector.tensor_scalar(
            one_plus[:].rearrange("p t j -> p (t j)"), ex[:].rearrange("p t j -> p (t j)"), EXP_CAP, 1.0, ALU.min, ALU.add
        )
        pieces = [(t, 0, J) for t in range(last)] + [(last, 0, HALF), (last, HALF, J)]
        for t, c0, c1 in pieces:
            soft = held.tile([P, c1 - c0], F32, name="soft%d_%d" % (t, c0))
            nc.scalar.activation(soft[:], one_plus[:, t, c0:c1], ACT.Ln)
            y = held.tile([P, c1 - c0], F32, name="y%d_%d" % (t, c0))
            nc.vector.scalar_tensor_tensor(y[:], z[:, t, c0:c1], margin[:, t : t + 1], soft[:], ALU.add, ALU.max)
            nc.sync.dma_start(out[t * P : (t + 1) * P, c0:c1], y[:])
